import numpy as np, ml_dtypes
CORES = [24,48,72,152,176,200]
N = 6
GR, GC = 2, 3
L, KA, KB, F = 6, 2, 3, 128
def setup_inputs(rng):
    return {"a": rng.standard_normal((N, 128, KA * 128), dtype=np.float32).astype(ml_dtypes.bfloat16), "b": rng.standard_normal((N, 128, KB * F), dtype=np.float32).astype(ml_dtypes.bfloat16)}
def setup_inputs_big(rng):
    d = setup_inputs(rng)
    for k in ("a", "b"): d[k] = (d[k].astype(np.float32) * 1024.0).astype(d[k].dtype)
    return d
def setup_inputs_small(rng):
    d = setup_inputs(rng)
    for k in ("a", "b"): d[k] = (d[k].astype(np.float32) * (1 / 1024.0)).astype(d[k].dtype)
    return d
def setup_inputs_apart(rng):
    d = setup_inputs(rng)
    f = (10.0 ** rng.permutation(np.linspace(-1.5, 1.5, N))).astype(np.float32).reshape(N, 1, 1)
    for k in ("a", "b"): d[k] = (d[k].astype(np.float32) * f).astype(d[k].dtype)
    return d
def reference(a, b):
    A, B = a.astype(np.float64), b.astype(np.float64)
    y = np.zeros((N, 128, F))
    for i in range(GR):
        for j in range(GC):
            for k in range(L):
                At = A[i * GC + k // KA][:, 128 * (k % KA):128 * (k % KA) + 128]
                Bt = B[(k // KB) * GC + j][:, F * (k % KB):F * (k % KB) + F]
                y[i * GC + j] += At.T @ Bt
    return {"y": y.astype(ml_dtypes.bfloat16 if a.dtype != np.float64 else np.float64)}

@@ -1,0 +1,139 @@
+from concourse.bass import DstId, RemoteDMATransfer
+
+GR, GC, L, KA, KB, F = 2, 3, 6, 2, 3, 128
+
+HOP1_ENGINES = 4
+SPREAD_DIES = True
+
+SCRATCH = {
+    "stage": ("dram", [128, KA * 128], "bfloat16"),
+    "A0": ("sbuf", [128, KA * 128], "bfloat16"),
+    "A1": ("sbuf", [128, KA * 128], "bfloat16"),
+    "A2": ("sbuf", [128, KA * 128], "bfloat16"),
+    "B0": ("sbuf", [128, KB * F], "bfloat16"),
+    "B1": ("sbuf", [128, KB * F], "bfloat16"),
+    "acc": ("psum", [128, F], "float32"),
+    "y_sb": ("sbuf", [128, F], "bfloat16"),
+}
+SEMAPHORES = ["ld_s", "ld_a", "ld_b", "in_r", "inA0", "inA1", "inA2", "inB", "sent", "mm", "cp", "st"]
+
+
+def _take(mask, n, skip=0):
+    bits = [1 << e for e in range(mask.bit_length()) if (mask >> e) & 1]
+    m = 0
+    for b in bits[skip:skip + n]:
+        m |= b
+    return m
+
+
+def _count(mask):
+    return sum((mask >> e) & 1 for e in range(mask.bit_length()))
+
+
+def _a_flows(T, topo):
+    cores = list(T.cores)
+    world = range(len({topo.host(c) for c in cores}) * topo.CORES_PER_HOST)
+    pairs = [(i, s, d) for i in range(GR) for s in range(GC) for d in range(GC) if s != d]
+    far = [(i, s, d) for (i, s, d) in pairs if not topo.may_write(cores[i * GC + s], cores[i * GC + d])]
+    flows, used = [], set()
+    for (i, s, d) in pairs:
+        src, dst = cores[i * GC + s], cores[i * GC + d]
+        if (i, s, d) not in far:
+            flows.append((src, dst, s, None, 0))
+            continue
+        n_out = [x for x in far if x[0] == i and x[1] == s].index((i, s, d))
+        n_in = [x for x in far if x[0] == i and x[2] == d].index((i, s, d))
+        lane = (n_out + n_in) % 2 if SPREAD_DIES else 0
+        can = [x for x in world if topo.host(x) == topo.host(src) and topo.chip(x) == topo.chip(src)
+               and x not in cores and x not in used and topo.may_write(x, dst)]
+        pool = [x for x in can if (topo.die(x) == topo.die(src)) == (lane == 0)]
+        used.add(pool[0])
+        flows.append((src, dst, s, pool[0], lane))
+    return flows
+
+
+def rank_program(g, core, T, topo):
+    sem = T.sem
+    flows = _a_flows(T, topo)
+    rank = T.rank_of(core)
+
+    if rank is None:
+        for (src, dst, s, relay, lane) in flows:
+            if relay != core:
+                continue
+            rid, pid = topo.addr(dst, core)
+            m = topo.mask(core, dst)
+            g.wait_ge(sem.in_r, HOP1_ENGINES)
+            g.remote_dma(out_ap=T["A%d" % s][:], in_ap=T.stage[:], remote_sem=sem["inA%d" % s], local_sem=sem.sent,
+                         pid=pid, routing_id=rid, dma_engine_mask=m)
+            g.wait_ge(sem.sent, _count(m))
+        return
+
+    row, col = rank // GC, rank % GC
+    cores = list(T.cores)
+    peer_b = cores[(1 - row) * GC + col]
+
+    g.sync.dma_start(T.stage[:], T.a[:]).then_inc(sem.ld_s, 16)
+    g.scalar.dma_start(T["B%d" % row][:], T.b[:]).then_inc(sem.ld_b, 16)
+    g.sync.dma_start(T["A%d" % col][:], T.a[:]).then_inc(sem.ld_a, 16)
+
+    mine = [f for f in flows if f[0] == core]
+    relayed = [f for f in mine if f[3] is not None]
+    direct = [f for f in mine if f[3] is None]
+    sent = 0
+
+    g.wait_ge(sem.ld_s, 16)
+    stay = topo.mask(core, relayed[0][3]) & ~topo.mask(core, peer_b)
+    trs = []
+    for n, (src, dst, s, relay, lane) in enumerate(relayed):
+        rid, pid = topo.addr(relay, core)
+        trs.append((rid, pid, _take(stay, HOP1_ENGINES, n * HOP1_ENGINES)))
+        sent += HOP1_ENGINES
+    if len(trs) == 1:
+        rid, pid, m = trs[0]
+        g.remote_dma(out_ap=T.stage[:], in_ap=T.stage[:], remote_sem=sem.in_r, local_sem=sem.sent,
+                     pid=pid, routing_id=rid, dma_engine_mask=m)
+    else:
+        g.remote_dma_fused([RemoteDMATransfer(dst_ids=[DstId(rid=rid, pnc=pid)], dma_engine_mask=m, remote_sem=sem.in_r,
+                                              src=T.stage[:], dst=T.stage[:]) for (rid, pid, m) in trs],
+                           local_sem=sem.sent)
+
+    for (src, dst, s, relay, lane) in direct:
+        rid, pid = topo.addr(dst, core)
+        m = topo.mask(core, dst)
+        g.remote_dma(out_ap=T["A%d" % s][:], in_ap=T.stage[:], remote_sem=sem["inA%d" % s], local_sem=sem.sent,
+                     pid=pid, routing_id=rid, dma_engine_mask=m)
+        sent += _count(m)
+    g.wait_ge(sem.ld_b, 16)
+    rid, pid = topo.addr(peer_b, core)
+    m = topo.mask(core, peer_b)
+    g.remote_dma(out_ap=T["B%d" % row][:], in_ap=T["B%d" % row][:], remote_sem=sem.inB, local_sem=sem.sent,
+                 pid=pid, routing_id=rid, dma_engine_mask=m)
+    sent += _count(m)
+    g.wait_ge(sem.sent, sent)
+
+    when_a, wait_a = {col: 0.0}, {col: (sem.ld_a, 16)}
+    for (src, dst, s, relay, lane) in flows:
+        if dst == core:
+            sender = src if relay is None else relay
+            when_a[s] = 1.0 if relay is None else 3.0 + lane
+            wait_a[s] = (sem["inA%d" % s], _count(topo.mask(sender, core)))
+    when_b = {row: 0.0, 1 - row: 2.0}
+    wait_b = {row: (sem.ld_b, 16), 1 - row: (sem.inB, _count(topo.mask(peer_b, core)))}
+
+    order = sorted(range(L), key=lambda k: (max(when_a[k // KA], when_b[k // KB]), k))
+    seen = set()
+    for n, k in enumerate(order):
+        for key, (s_, v_) in (("a%d" % (k // KA), wait_a[k // KA]), ("b%d" % (k // KB), wait_b[k // KB])):
+            if key not in seen:
+                seen.add(key)
+                g.tensor.wait_ge(s_, v_)
+        ta, tb = k % KA, k % KB
+        g.tensor.matmul(T.acc[:], T["A%d" % (k // KA)][:, 128 * ta:128 * ta + 128], T["B%d" % (k // KB)][:, F * tb:F * tb + F],
+                        n == 0, n == L - 1).then_inc(sem.mm, 1)
+
+    g.vector.wait_ge(sem.mm, L)
+    g.vector.tensor_copy(T.y_sb[:], T.acc[:]).then_inc(sem.cp, 1)
+    g.sync.wait_ge(sem.cp, 1)
+    g.sync.dma_start(T.y[:], T.y_sb[:]).then_inc(sem.st, 16)
+    g.sync.wait_ge(sem.st, 16)

@@ -1,54 +1,60 @@
 from concourse.bass import DstId, RemoteDMATransfer
 
 GR, GC, L, KA, KB, F = 2, 3, 6, 2, 3, 128
+H = F // 2
 
 HOP1_ENGINES = 4
-SPREAD_DIES = True
 
 SCRATCH = {
-    "stage": ("dram", [128, KA * 128], "bfloat16"),
+    "stage0": ("dram", [128, 128], "bfloat16"),
+    "stage1": ("dram", [128, 128], "bfloat16"),
     "A0": ("sbuf", [128, KA * 128], "bfloat16"),
     "A1": ("sbuf", [128, KA * 128], "bfloat16"),
     "A2": ("sbuf", [128, KA * 128], "bfloat16"),
     "B0": ("sbuf", [128, KB * F], "bfloat16"),
     "B1": ("sbuf", [128, KB * F], "bfloat16"),
-    "acc": ("psum", [128, F], "float32"),
+    "acc0": ("psum", [128, 512], "float32"),
+    "acc1": ("psum", [128, 512], "float32"),
     "y_sb": ("sbuf", [128, F], "bfloat16"),
 }
-SEMAPHORES = ["ld_s", "ld_a", "ld_b", "in_r", "inA0", "inA1", "inA2", "inB", "sent", "mm", "cp", "st"]
+SEMAPHORES = (["ld_s0", "ld_s1", "ld_a", "ld_b", "in_r", "inB", "sent", "mm0", "mm1", "cp", "st"]
+              + ["inA%d_%d" % (s, t) for s in range(GC) for t in range(KA)])
 
 
-def _take(mask, n, skip=0):
-    bits = [1 << e for e in range(mask.bit_length()) if (mask >> e) & 1]
+def _bits(mask):
+    return [1 << e for e in range(mask.bit_length()) if (mask >> e) & 1]
+
+
+def _join(bits):
     m = 0
-    for b in bits[skip:skip + n]:
+    for b in bits:
         m |= b
     return m
 
 
 def _count(mask):
-    return sum((mask >> e) & 1 for e in range(mask.bit_length()))
+    return len(_bits(mask))
 
 
 def _a_flows(T, topo):
     cores = list(T.cores)
     world = range(len({topo.host(c) for c in cores}) * topo.CORES_PER_HOST)
-    pairs = [(i, s, d) for i in range(GR) for s in range(GC) for d in range(GC) if s != d]
-    far = [(i, s, d) for (i, s, d) in pairs if not topo.may_write(cores[i * GC + s], cores[i * GC + d])]
     flows, used = [], set()
-    for (i, s, d) in pairs:
-        src, dst = cores[i * GC + s], cores[i * GC + d]
-        if (i, s, d) not in far:
-            flows.append((src, dst, s, None, 0))
-            continue
-        n_out = [x for x in far if x[0] == i and x[1] == s].index((i, s, d))
-        n_in = [x for x in far if x[0] == i and x[2] == d].index((i, s, d))
-        lane = (n_out + n_in) % 2 if SPREAD_DIES else 0
-        can = [x for x in world if topo.host(x) == topo.host(src) and topo.chip(x) == topo.chip(src)
-               and x not in cores and x not in used and topo.may_write(x, dst)]
-        pool = [x for x in can if (topo.die(x) == topo.die(src)) == (lane == 0)]
-        used.add(pool[0])
-        flows.append((src, dst, s, pool[0], lane))
+    for i in range(GR):
+        for s in range(GC):
+            for d in range(GC):
+                if s == d:
+                    continue
+                src, dst = cores[i * GC + s], cores[i * GC + d]
+                if topo.may_write(src, dst):
+                    flows.append((src, dst, s, None, None))
+                    continue
+                for t in range(KA):
+                    pool = [x for x in world if topo.host(x) == topo.host(src) and topo.chip(x) == topo.chip(src)
+                            and x not in cores and x not in used and topo.may_write(x, dst)
+                            and (topo.die(x) == topo.die(src)) == (t == KA - 1)]
+                    used.add(pool[0])
+                    flows.append((src, dst, s, t, pool[0]))
     return flows
 
 
@@ -58,14 +64,14 @@ def rank_program(g, core, T, topo):
     rank = T.rank_of(core)
 
     if rank is None:
-        for (src, dst, s, relay, lane) in flows:
-            if relay != core:
+        for (src, dst, s, t, helper) in flows:
+            if helper != core:
                 continue
             rid, pid = topo.addr(dst, core)
             m = topo.mask(core, dst)
             g.wait_ge(sem.in_r, HOP1_ENGINES)
-            g.remote_dma(out_ap=T["A%d" % s][:], in_ap=T.stage[:], remote_sem=sem["inA%d" % s], local_sem=sem.sent,
-                         pid=pid, routing_id=rid, dma_engine_mask=m)
+            g.remote_dma(out_ap=T["A%d" % s][:, 128 * t:128 * t + 128], in_ap=T["stage%d" % t][:],
+                         remote_sem=sem["inA%d_%d" % (s, t)], local_sem=sem.sent, pid=pid, routing_id=rid, dma_engine_mask=m)
             g.wait_ge(sem.sent, _count(m))
         return
 
@@ -73,67 +79,81 @@ def rank_program(g, core, T, topo):
     cores = list(T.cores)
     peer_b = cores[(1 - row) * GC + col]
 
-    g.sync.dma_start(T.stage[:], T.a[:]).then_inc(sem.ld_s, 16)
-    g.scalar.dma_start(T["B%d" % row][:], T.b[:]).then_inc(sem.ld_b, 16)
+    for t in range(KA):
+        g.sync.dma_start(T["stage%d" % t][:], T.a[:, 128 * t:128 * t + 128]).then_inc(sem["ld_s%d" % t], 16)
+    g.sync.dma_start(T["B%d" % row][:], T.b[:]).then_inc(sem.ld_b, 16)
     g.sync.dma_start(T["A%d" % col][:], T.a[:]).then_inc(sem.ld_a, 16)
 
     mine = [f for f in flows if f[0] == core]
-    relayed = [f for f in mine if f[3] is not None]
-    direct = [f for f in mine if f[3] is None]
+    direct = [f for f in mine if f[4] is None]
     sent = 0
 
-    g.wait_ge(sem.ld_s, 16)
-    stay = topo.mask(core, relayed[0][3]) & ~topo.mask(core, peer_b)
-    trs = []
-    for n, (src, dst, s, relay, lane) in enumerate(relayed):
-        rid, pid = topo.addr(relay, core)
-        trs.append((rid, pid, _take(stay, HOP1_ENGINES, n * HOP1_ENGINES)))
-        sent += HOP1_ENGINES
-    if len(trs) == 1:
-        rid, pid, m = trs[0]
-        g.remote_dma(out_ap=T.stage[:], in_ap=T.stage[:], remote_sem=sem.in_r, local_sem=sem.sent,
-                     pid=pid, routing_id=rid, dma_engine_mask=m)
-    else:
-        g.remote_dma_fused([RemoteDMATransfer(dst_ids=[DstId(rid=rid, pnc=pid)], dma_engine_mask=m, remote_sem=sem.in_r,
-                                              src=T.stage[:], dst=T.stage[:]) for (rid, pid, m) in trs],
-                           local_sem=sem.sent)
+    for t in range(KA):
+        part = [f for f in mine if f[3] == t]
+        stay = _bits(topo.mask(core, part[0][4]) & ~topo.mask(core, peer_b))
+        step = len(stay) // (HOP1_ENGINES * len(part))
+        trs = []
+        for n, (src, dst, s, t_, helper) in enumerate(part):
+            rid, pid = topo.addr(helper, core)
+            trs.append((rid, pid, _join(stay[n * HOP1_ENGINES * step:(n + 1) * HOP1_ENGINES * step:step])))
+            sent += HOP1_ENGINES
+        st = T["stage%d" % t]
+        g.wait_ge(sem["ld_s%d" % t], 16)
+        if len(trs) == 1:
+            rid, pid, m = trs[0]
+            g.remote_dma(out_ap=st[:], in_ap=st[:], remote_sem=sem.in_r, local_sem=sem.sent,
+                         pid=pid, routing_id=rid, dma_engine_mask=m)
+        else:
+            g.remote_dma_fused([RemoteDMATransfer(dst_ids=[DstId(rid=rid, pnc=pid)], dma_engine_mask=m, remote_sem=sem.in_r,
+                                                  src=st[:], dst=st[:]) for (rid, pid, m) in trs],
+                               local_sem=sem.sent)
 
-    for (src, dst, s, relay, lane) in direct:
-        rid, pid = topo.addr(dst, core)
-        m = topo.mask(core, dst)
-        g.remote_dma(out_ap=T["A%d" % s][:], in_ap=T.stage[:], remote_sem=sem["inA%d" % s], local_sem=sem.sent,
-                     pid=pid, routing_id=rid, dma_engine_mask=m)
-        sent += _count(m)
     g.wait_ge(sem.ld_b, 16)
     rid, pid = topo.addr(peer_b, core)
     m = topo.mask(core, peer_b)
     g.remote_dma(out_ap=T["B%d" % row][:], in_ap=T["B%d" % row][:], remote_sem=sem.inB, local_sem=sem.sent,
                  pid=pid, routing_id=rid, dma_engine_mask=m)
     sent += _count(m)
+    if direct:
+        g.wait_ge(sem.ld_a, 16)
+    for (src, dst, s, t, helper) in direct:
+        rid, pid = topo.addr(dst, core)
+        m = topo.mask(core, dst)
+        g.remote_dma(out_ap=T["A%d" % s][:], in_ap=T["A%d" % s][:], remote_sem=sem["inA%d_0" % s], local_sem=sem.sent,
+                     pid=pid, routing_id=rid, dma_engine_mask=m)
+        sent += _count(m)
     g.wait_ge(sem.sent, sent)
 
-    when_a, wait_a = {col: 0.0}, {col: (sem.ld_a, 16)}
-    for (src, dst, s, relay, lane) in flows:
-        if dst == core:
-            sender = src if relay is None else relay
-            when_a[s] = 1.0 if relay is None else 3.0 + lane
-            wait_a[s] = (sem["inA%d" % s], _count(topo.mask(sender, core)))
-    when_b = {row: 0.0, 1 - row: 2.0}
-    wait_b = {row: (sem.ld_b, 16), 1 - row: (sem.inB, _count(topo.mask(peer_b, core)))}
+    when_a, wait_a = {}, {}
+    for t in range(KA):
+        when_a[col * KA + t], wait_a[col * KA + t] = 0.0, ("ld_a", 16)
+    for (src, dst, s, t, helper) in flows:
+        if dst != core:
+            continue
+        if helper is None:
+            for t_ in range(KA):
+                when_a[s * KA + t_], wait_a[s * KA + t_] = 2.0, ("inA%d_0" % s, _count(topo.mask(src, core)))
+        else:
+            when_a[s * KA + t], wait_a[s * KA + t] = 3.0 + t, ("inA%d_%d" % (s, t), _count(topo.mask(helper, core)))
+    when_b = {row: 0.0, 1 - row: 1.0}
+    wait_b = {row: ("ld_b", 16), 1 - row: ("inB", _count(topo.mask(peer_b, core)))}
 
-    order = sorted(range(L), key=lambda k: (max(when_a[k // KA], when_b[k // KB]), k))
+    order = sorted(range(L), key=lambda k: (max(when_a[k], when_b[k // KB]), k))
     seen = set()
     for n, k in enumerate(order):
-        for key, (s_, v_) in (("a%d" % (k // KA), wait_a[k // KA]), ("b%d" % (k // KB), wait_b[k // KB])):
-            if key not in seen:
-                seen.add(key)
-                g.tensor.wait_ge(s_, v_)
+        for (name, v) in (wait_a[k], wait_b[k // KB]):
+            if name not in seen:
+                seen.add(name)
+                g.tensor.wait_ge(sem[name], v)
         ta, tb = k % KA, k % KB
-        g.tensor.matmul(T.acc[:], T["A%d" % (k // KA)][:, 128 * ta:128 * ta + 128], T["B%d" % (k // KB)][:, F * tb:F * tb + F],
-                        n == 0, n == L - 1).then_inc(sem.mm, 1)
+        for h in range(2):
+            g.tensor.matmul(T["acc%d" % h][:, 0:H], T["A%d" % (k // KA)][:, 128 * ta:128 * ta + 128],
+                            T["B%d" % (k // KB)][:, F * tb + H * h:F * tb + H * h + H],
+                            n == 0, n == L - 1).then_inc(sem["mm%d" % h], 1)
 
-    g.vector.wait_ge(sem.mm, L)
-    g.vector.tensor_copy(T.y_sb[:], T.acc[:]).then_inc(sem.cp, 1)
-    g.sync.wait_ge(sem.cp, 1)
+    for h in range(2):
+        g.vector.wait_ge(sem["mm%d" % h], L)
+        g.vector.tensor_copy(T.y_sb[:, H * h:H * h + H], T["acc%d" % h][:, 0:H]).then_inc(sem.cp, 1)
+    g.sync.wait_ge(sem.cp, 2)
     g.sync.dma_start(T.y[:], T.y_sb[:]).then_inc(sem.st, 16)
     g.sync.wait_ge(sem.st, 16)

from concourse.bass import DstId, RemoteDMATransfer

GR, GC, L, KA, KB, F = 2, 3, 6, 2, 3, 128
H = F // 2

HOP1_ENGINES = 4

SCRATCH = {
    "stage0": ("dram", [128, 128], "bfloat16"),
    "stage1": ("dram", [128, 128], "bfloat16"),
    "A0": ("sbuf", [128, KA * 128], "bfloat16"),
    "A1": ("sbuf", [128, KA * 128], "bfloat16"),
    "A2": ("sbuf", [128, KA * 128], "bfloat16"),
    "B0": ("sbuf", [128, KB * F], "bfloat16"),
    "B1": ("sbuf", [128, KB * F], "bfloat16"),
    "acc0": ("psum", [128, 512], "float32"),
    "acc1": ("psum", [128, 512], "float32"),
    "y_sb": ("sbuf", [128, F], "bfloat16"),
}
SEMAPHORES = (["ld_s0", "ld_s1", "ld_a", "ld_b", "in_r", "inB", "sent", "mm0", "mm1", "cp", "st"]
              + ["inA%d_%d" % (s, t) for s in range(GC) for t in range(KA)])


def _bits(mask):
    return [1 << e for e in range(mask.bit_length()) if (mask >> e) & 1]


def _join(bits):
    m = 0
    for b in bits:
        m |= b
    return m


def _count(mask):
    return len(_bits(mask))


def _a_flows(T, topo):
    cores = list(T.cores)
    world = range(len({topo.host(c) for c in cores}) * topo.CORES_PER_HOST)
    flows, used = [], set()
    for i in range(GR):
        for s in range(GC):
            for d in range(GC):
                if s == d:
                    continue
                src, dst = cores[i * GC + s], cores[i * GC + d]
                if topo.may_write(src, dst):
                    flows.append((src, dst, s, None, None))
                    continue
                for t in range(KA):
                    pool = [x for x in world if topo.host(x) == topo.host(src) and topo.chip(x) == topo.chip(src)
                            and x not in cores and x not in used and topo.may_write(x, dst)
                            and (topo.die(x) == topo.die(src)) == (t == KA - 1)]
                    used.add(pool[0])
                    flows.append((src, dst, s, t, pool[0]))
    return flows


def rank_program(g, core, T, topo):
    sem = T.sem
    flows = _a_flows(T, topo)
    rank = T.rank_of(core)

    if rank is None:
        for (src, dst, s, t, helper) in flows:
            if helper != core:
                continue
            rid, pid = topo.addr(dst, core)
            m = topo.mask(core, dst)
            g.wait_ge(sem.in_r, HOP1_ENGINES)
            g.remote_dma(out_ap=T["A%d" % s][:, 128 * t:128 * t + 128], in_ap=T["stage%d" % t][:],
                         remote_sem=sem["inA%d_%d" % (s, t)], local_sem=sem.sent, pid=pid, routing_id=rid, dma_engine_mask=m)
            g.wait_ge(sem.sent, _count(m))
        return

    row, col = rank // GC, rank % GC
    cores = list(T.cores)
    peer_b = cores[(1 - row) * GC + col]

    for t in range(KA):
        g.sync.dma_start(T["stage%d" % t][:], T.a[:, 128 * t:128 * t + 128]).then_inc(sem["ld_s%d" % t], 16)
    g.sync.dma_start(T["B%d" % row][:], T.b[:]).then_inc(sem.ld_b, 16)
    g.sync.dma_start(T["A%d" % col][:], T.a[:]).then_inc(sem.ld_a, 16)

    mine = [f for f in flows if f[0] == core]
    direct = [f for f in mine if f[4] is None]
    sent = 0

    for t in range(KA):
        part = [f for f in mine if f[3] == t]
        stay = _bits(topo.mask(core, part[0][4]) & ~topo.mask(core, peer_b))
        step = len(stay) // (HOP1_ENGINES * len(part))
        trs = []
        for n, (src, dst, s, t_, helper) in enumerate(part):
            rid, pid = topo.addr(helper, core)
            trs.append((rid, pid, _join(stay[n * HOP1_ENGINES * step:(n + 1) * HOP1_ENGINES * step:step])))
            sent += HOP1_ENGINES
        st = T["stage%d" % t]
        g.wait_ge(sem["ld_s%d" % t], 16)
        if len(trs) == 1:
            rid, pid, m = trs[0]
            g.remote_dma(out_ap=st[:], in_ap=st[:], remote_sem=sem.in_r, local_sem=sem.sent,
                         pid=pid, routing_id=rid, dma_engine_mask=m)
        else:
            g.remote_dma_fused([RemoteDMATransfer(dst_ids=[DstId(rid=rid, pnc=pid)], dma_engine_mask=m, remote_sem=sem.in_r,
                                                  src=st[:], dst=st[:]) for (rid, pid, m) in trs],
                               local_sem=sem.sent)

    g.wait_ge(sem.ld_b, 16)
    rid, pid = topo.addr(peer_b, core)
    m = topo.mask(core, peer_b)
    g.remote_dma(out_ap=T["B%d" % row][:], in_ap=T["B%d" % row][:], remote_sem=sem.inB, local_sem=sem.sent,
                 pid=pid, routing_id=rid, dma_engine_mask=m)
    sent += _count(m)
    if direct:
        g.wait_ge(sem.ld_a, 16)
    for (src, dst, s, t, helper) in direct:
        rid, pid = topo.addr(dst, core)
        m = topo.mask(core, dst)
        g.remote_dma(out_ap=T["A%d" % s][:], in_ap=T["A%d" % s][:], remote_sem=sem["inA%d_0" % s], local_sem=sem.sent,
                     pid=pid, routing_id=rid, dma_engine_mask=m)
        sent += _count(m)
    g.wait_ge(sem.sent, sent)

    when_a, wait_a = {}, {}
    for t in range(KA):
        when_a[col * KA + t], wait_a[col * KA + t] = 0.0, ("ld_a", 16)
    for (src, dst, s, t, helper) in flows:
        if dst != core:
            continue
        if helper is None:
            for t_ in range(KA):
                when_a[s * KA + t_], wait_a[s * KA + t_] = 2.0, ("inA%d_0" % s, _count(topo.mask(src, core)))
        else:
            when_a[s * KA + t], wait_a[s * KA + t] = 3.0 + t, ("inA%d_%d" % (s, t), _count(topo.mask(helper, core)))
    when_b = {row: 0.0, 1 - row: 1.0}
    wait_b = {row: ("ld_b", 16), 1 - row: ("inB", _count(topo.mask(peer_b, core)))}

    order = sorted(range(L), key=lambda k: (max(when_a[k], when_b[k // KB]), k))
    seen = set()
    for n, k in enumerate(order):
        for (name, v) in (wait_a[k], wait_b[k // KB]):
            if name not in seen:
                seen.add(name)
                g.tensor.wait_ge(sem[name], v)
        ta, tb = k % KA, k % KB
        for h in range(2):
            g.tensor.matmul(T["acc%d" % h][:, 0:H], T["A%d" % (k // KA)][:, 128 * ta:128 * ta + 128],
                            T["B%d" % (k // KB)][:, F * tb + H * h:F * tb + H * h + H],
                            n == 0, n == L - 1).then_inc(sem["mm%d" % h], 1)

    for h in range(2):
        g.vector.wait_ge(sem["mm%d" % h], L)
        g.vector.tensor_copy(T.y_sb[:, H * h:H * h + H], T["acc%d" % h][:, 0:H]).then_inc(sem.cp, 1)
    g.sync.wait_ge(sem.cp, 2)
    g.sync.dma_start(T.y[:], T.y_sb[:]).then_inc(sem.st, 16)
    g.sync.wait_ge(sem.st, 16)
